import numpy as np
import ml_dtypes


def mxq(x, axis, fmt="e4m3"):
    dtype, down = {"e4m3": (ml_dtypes.float8_e4m3fn, 7), "e5m2": (ml_dtypes.float8_e5m2, 14)}[fmt]
    v = np.moveaxis(np.asarray(x, np.float32).astype(ml_dtypes.bfloat16).astype(np.float64), axis, -1)
    blocks = v.reshape(v.shape[:-1] + (-1, 32))
    amax = np.abs(blocks).max(-1, keepdims=True)
    byte = np.maximum(np.where(amax > 0, np.frexp(amax)[1] - 1 + 127, 0) - down, 1)
    scale = np.exp2(byte - 127.0)
    codes = (blocks / scale).astype(np.float32).astype(dtype).astype(np.float64)
    return np.moveaxis((codes * scale).reshape(v.shape), -1, axis)


WIDE = False


def mx_kscale(k):
    if not WIDE:
        return np.ones(k)
    levels = np.array([10, -10, 5, -5, 0])
    if k % 512:
        return np.exp2(np.random.permutation(np.resize(levels, k // 32))).repeat(32)
    a = np.empty((k // 512, 16))
    for p in range(k // 512):
        a[p, :8] = np.random.permutation(np.resize(levels, 8))
        for g in range(8):
            far = levels[np.abs(levels - a[p, g]) >= 10]
            a[p, g + 8] = far[np.random.randint(len(far))]
    return np.exp2(a.ravel()).repeat(32)


def f64(x):
    return np.asarray(x).astype(np.float64)


def striped(idx):
    return np.tile(idx.reshape(-1, 16).T, (8, 1)).astype(np.uint16)


def unstriped(offs):
    return offs[:16].T.reshape(-1).astype(np.int64)


def striped8(idx):
    return np.concatenate([x.reshape(-1, 16).T for x in idx]).astype(np.uint16)


def runs(offs, k):
    lists = np.stack([offs[16 * r : 16 * r + 16].T.reshape(-1) for r in range(8)]).astype(np.int64)
    return lists[np.arange(k) % 512 // 64]


def pack_weight(w):
    k, n = w.shape
    w = f64(np.asarray(w, np.float32).astype(ml_dtypes.bfloat16)).reshape(k // 32, 32, n)
    amax = np.abs(w).max(1)
    byte = np.clip(np.where(amax > 0, np.frexp(amax)[1] - 1 + 127 - 7, 1), 1, 254)
    scaled = (w * np.exp2(127.0 - byte)[:, None, :]).reshape(k, n).astype(np.float32)
    words = np.ascontiguousarray(scaled.reshape(k // 512, 128, 4, n).transpose(0, 1, 3, 2)).astype(ml_dtypes.float8_e4m3fn).view(np.uint8)
    return words, np.ascontiguousarray(byte.astype(np.uint8).reshape(k // 512, 16, n))


def unpack_weight(words, scales):
    g, p, n, _ = words.shape
    vals = np.ascontiguousarray(words).view(ml_dtypes.float8_e4m3fn).astype(np.float64) * np.repeat(np.exp2(scales.astype(np.float64) - 127.0), 8, axis=1)[..., None]
    return vals.transpose(0, 1, 3, 2).reshape(g * 512, n)


def sigmoid(v):
    return 1.0 / (1.0 + np.exp(-np.maximum(v, -700.0)))

def planes(y):
    n, m = y.shape
    v = y.astype(np.float32).astype(ml_dtypes.bfloat16).astype(np.float64).reshape(n // 32, 32, m)
    top = np.abs(v).max(1)
    byte = np.clip(np.where(top > 0, np.frexp(top)[1] - 1 + 127 - 7, 1), 1, 254)
    codes = (v * np.exp2(127.0 - byte)[:, None, :]).reshape(n, m).astype(np.float32).astype(ml_dtypes.float8_e4m3fn).view(np.uint8)
    words = codes.reshape(n // 512, 128, 4, m).transpose(0, 1, 3, 2)
    return np.ascontiguousarray(words), np.ascontiguousarray(byte.astype(np.uint8).reshape(n // 512, 16, m))


K, T, S, G, H, W = 512, 1024, 512, 2048, 512, 256


def setup_inputs():
    n = np.random.standard_normal
    s = mx_kscale(K)[:, None]
    packed_xT = pack_weight(n((K, T)) * s)
    packed_dT = pack_weight(n((K, G)) / s)
    perm = np.stack([np.random.permutation(S) for _ in range(8)])
    return {
        "x_words": packed_xT[0],
        "x_scales": packed_xT[1],
        "d_words": packed_dT[0],
        "d_scales": packed_dT[1],
        "gs": (np.random.uniform(0.5, 1.5, (K, 1)) * s).astype(np.float32),
        "offs": striped(np.random.permutation(T)[:S]),
        "k1": striped8(np.random.randint(0, G, (8, H))),
        "n1": striped8(perm[:, :W]),
        "n2": striped8(perm[:, W:]),
        "k2": striped8(np.random.randint(0, G, (8, H))),
        "n3": striped8(np.stack([np.random.permutation(S) for _ in range(8)])),
        "n4": striped8(np.stack([np.random.permutation(S) for _ in range(8)])),
    }


def reference(x_words, x_scales, d_words, d_scales, gs, offs, k1, n1, n2, k2, n3, n4):
    d_k2 = unpack_weight(d_words, d_scales)[np.arange(K)[:, None], runs(k2, K)]
    d_k1 = unpack_weight(d_words, d_scales)[np.arange(K)[:, None], runs(k1, K)]
    xq = unpack_weight(x_words, x_scales)[:, unstriped(offs)]
    h = 0.0625 * (d_k1.T @ xq)
    pa = h[np.arange(H)[:, None], runs(n1, H)]
    pb = h[np.arange(H)[:, None], runs(n2, H)]
    rb = pa * pb
    ra = pa + pb
    ds = np.zeros((H, S))
    ds[np.arange(H)[:, None], runs(n1, H)] = ra
    dt = ds.copy()
    dt[np.arange(H)[:, None], runs(n2, H)] = rb
    z = f64(gs) * dt
    h2 = 0.0625 * ((d_k2.T @ mxq(z, 0, "e4m3")))
    st = h2 * (sigmoid(h2[np.arange(H)[:, None], runs(n3, H)]))
    out_0 = st - (st[np.arange(H)[:, None], runs(n4, H)])
    return (out_0,) + planes(out_0)

@@ -1,0 +1,238 @@
+from contextlib import ExitStack
+
+import concourse.mybir as mybir
+
+F32 = mybir.dt.float32
+BF16 = mybir.dt.bfloat16
+I32 = mybir.dt.int32
+U32 = mybir.dt.uint32
+U16 = mybir.dt.uint16
+U8 = mybir.dt.uint8
+FP8X4 = mybir.dt.float8_e4m3fn_x4
+ALU = mybir.AluOpType
+ACT = mybir.ActivationFunctionType
+
+P = 128
+PACK = 4
+T, G, S, W = 1024, 2048, 512, 256
+FLOPS = 2 * 2 * 512 * 512 * 512
+HALF = S // 2
+CHUNKS = ((0, 256), (256, 384), (384, 512))
+
+
+def tile_picked_codebondhopg_none_po_kernel(
+    tc, x_words, x_scales, d_words, d_scales, gs, offs, k1, n1, n2, k2, n3, n4, out_0, out_1, out_2
+):
+    nc = tc.nc
+    with ExitStack() as ctx:
+        keep = ctx.enter_context(tc.tile_pool(name="keep", bufs=1))
+        psum = ctx.enter_context(tc.psum_pool(name="psum", bufs=1))
+
+        def load_list(name, src):
+            tile = keep.tile(list(src.shape), U16, name=name)
+            nc.sync.dma_start(tile[:], src)
+            return tile
+
+        def entries(lst, lo, hi):
+            return lst[:, lo // 16 : hi // 16]
+
+        def zeroed_bytes(name, width):
+            tile = keep.tile([P, width], U8, name=name, align_bytes=64)
+            nc.vector.memset(tile[:].bitcast(I32), 0)
+            return tile
+
+        def move_rows(dst, src):
+            for j in range(4):
+                queue = nc.sync if j % 2 else nc.scalar
+                queue.dma_start(dst[j:P:32, :].bitcast(I32), src[8 * j : P : 32, :].bitcast(I32))
+
+        def deal_words(dst, src):
+            nc.vector.tensor_copy(
+                dst[:].bitcast(U32).rearrange("p (t c i) -> p c t i", t=PACK, i=4),
+                src[:].bitcast(U32).rearrange("p (c i t) -> p c t i", t=PACK, i=4),
+            )
+
+        def deal_bytes(dst, src):
+            nc.vector.tensor_copy(
+                dst.rearrange("p (t m) -> p m t", t=PACK),
+                src.rearrange("p (m t) -> p m t", t=PACK),
+            )
+
+        xs_win = zeroed_bytes("xs_win", T)
+        ds_win = zeroed_bytes("ds_win", G)
+        nc.scalar.dma_start(xs_win[0:P:8, :].bitcast(I32), x_scales[0].bitcast(I32))
+        nc.scalar.dma_start(ds_win[0:P:8, :].bitcast(I32), d_scales[0].bitcast(I32))
+        offs_t = load_list("offs_t", offs)
+        k1_t = load_list("k1_t", k1)
+        k2_t = load_list("k2_t", k2)
+        n1_t = load_list("n1_t", n1)
+        n2_t = load_list("n2_t", n2)
+        xw_win = keep.tile([P, T], I32, name="xw_win")
+        nc.sync.dma_start(xw_win[:], x_words[0].rearrange("p n t -> p (n t)").bitcast(I32))
+        dw_win = keep.tile([P, G], I32, name="dw_win")
+        nc.sync.dma_start(dw_win[:], d_words[0].rearrange("p n t -> p (n t)").bitcast(I32))
+        n3_t = load_list("n3_t", n3)
+        n4_t = load_list("n4_t", n4)
+        gs_t = keep.tile([P, PACK], F32, name="gs_t")
+        nc.gpsimd.dma_start(gs_t[:], gs.rearrange("(p t) o -> p (t o)", t=PACK))
+        planes1 = zeroed_bytes("planes1", 2 * S)
+        planes2 = zeroed_bytes("planes2", S)
+        warm = keep.tile([P, 2], F32, name="warm")
+        nc.vector.memset(warm[:, 0:1], 0.0)
+        nc.scalar.activation(warm[:, 1:2], warm[:, 0:1], ACT.Sigmoid)
+
+        picked1 = keep.tile([P, 2 * S], U8, name="picked1")
+        nc.vector.tensor_copy(picked1[:, S:], xs_win[:].indirect(offs_t[:]))
+        nc.vector.tensor_copy(picked1[:, :S], ds_win[:].indirect(k1_t[:]))
+        move_rows(planes1, picked1)
+        xq = keep.tile([P, S], I32, name="xq", align_bytes=64)
+        nc.vector.tensor_copy(xq[:].bitcast(U32), xw_win[:].bitcast(U32).indirect(offs_t[:]))
+        d1_raw = keep.tile([P, S], I32, name="d1_raw", tag="d1_raw")
+        nc.vector.tensor_copy(d1_raw[:].bitcast(U32), dw_win[:].bitcast(U32).indirect(k1_t[:]))
+        d1 = keep.tile([P, S], I32, name="d1", align_bytes=64)
+        deal_words(d1, d1_raw)
+        d1_scale = keep.tile([P, S], U8, name="d1_scale", align_bytes=64)
+        deal_bytes(d1_scale[:], planes1[:, :S])
+
+        picked2 = keep.tile([P, S], U8, name="picked2", tag="d1_raw")
+        nc.vector.tensor_copy(picked2[:], ds_win[:].indirect(k2_t[:]))
+        move_rows(planes2, picked2)
+
+        h = []
+        for t in range(PACK):
+            cols = slice(t * P, (t + 1) * P)
+            acc = psum.tile([P, S], F32, name=f"acc1_{t}")
+            nc.tensor.matmul_mx(
+                acc[:], lhsT=d1[:, cols].bitcast(FP8X4), lhsT_scale=d1_scale[:, cols],
+                rhs=xq[:].bitcast(FP8X4), rhs_scale=planes1[:, S:], start=True, stop=True,
+            )
+            h_t = keep.tile([P, S], F32, name=f"h{t}")
+            nc.scalar.activation(h_t[:], acc[:], ACT.Copy, scale=0.0625)
+            h.append(h_t)
+
+        pa = [keep.tile([P, W], F32, name=f"pa{t}", tag=f"pa{t}") for t in range(PACK)]
+        pb = [keep.tile([P, W], F32, name=f"pb{t}", tag=f"pb{t}", align_bytes=64) for t in range(PACK)]
+        dt = [keep.tile([P, S], F32, name=f"dt{t}") for t in range(PACK)]
+        z = [keep.tile([P, HALF, PACK], BF16, name=f"z{u}", align_bytes=64) for u in range(2)]
+
+        def fetch_a(t):
+            nc.vector.tensor_copy(pa[t][:], h[t][:].indirect(n1_t[:]))
+
+        def fetch_b(t):
+            nc.vector.tensor_copy(pb[t][:], h[t][:].indirect(n2_t[:]))
+
+        def put_sum(t):
+            nc.vector.tensor_tensor(dt[t][:].indirect(n1_t[:]), pa[t][:], pb[t][:], ALU.add)
+
+        def put_product(t):
+            nc.vector.tensor_tensor(dt[t][:].indirect(n2_t[:]), pa[t][:], pb[t][:], ALU.mult)
+            for u in range(2):
+                nc.scalar.activation(
+                    z[u][:, :, t], dt[t][:, u * HALF : (u + 1) * HALF], ACT.Copy, scale=gs_t[:, t : t + 1]
+                )
+
+        fetch_a(0)
+        fetch_b(0)
+        fetch_a(1)
+        put_sum(0)
+        fetch_b(1)
+        put_product(0)
+        fetch_a(2)
+        put_sum(1)
+        fetch_b(2)
+        put_product(1)
+        fetch_a(3)
+        put_sum(2)
+        fetch_b(3)
+        put_product(2)
+        put_sum(3)
+        put_product(3)
+
+        d2_raw = keep.tile([P, S], I32, name="d2_raw", tag="pa3")
+        nc.vector.tensor_copy(d2_raw[:].bitcast(U32), dw_win[:].bitcast(U32).indirect(k2_t[:]))
+        d2_scale = keep.tile([P, S], U8, name="d2_scale", tag="pb3", align_bytes=64)
+        deal_bytes(d2_scale[:], planes2[:])
+        d2 = keep.tile([P, S], I32, name="d2", align_bytes=64)
+        deal_words(d2, d2_raw)
+        zq = keep.tile([P, S], I32, name="zq", align_bytes=64)
+        zs = keep.tile([P, S], U8, name="zs", align_bytes=64)
+        for u in range(2):
+            cols = slice(u * HALF, (u + 1) * HALF)
+            nc.vector.quantize_mx(zq[:, cols].bitcast(FP8X4), zs[:, cols], z[u][:].rearrange("p c t -> p (c t)"))
+
+        h2 = [keep.tile([P, S], F32, name=f"h2_{t}") for t in range(PACK)]
+        for t in range(PACK):
+            cols = slice(t * P, (t + 1) * P)
+            acc = psum.tile([P, S], F32, name=f"acc2_{t}")
+            nc.tensor.matmul_mx(
+                acc[:], lhsT=d2[:, cols].bitcast(FP8X4), lhsT_scale=d2_scale[:, cols],
+                rhs=zq[:].bitcast(FP8X4), rhs_scale=zs[:], start=True, stop=True,
+            )
+            if t == 0:
+                nc.scalar.activation(h2[t][:], acc[:], ACT.Copy, scale=0.0625)
+            else:
+                nc.vector.tensor_scalar(h2[t][:], acc[:], 0.0625, None, ALU.mult)
+
+        gate = [keep.tile([P, S], F32, name=f"gate{t}") for t in range(PACK)]
+        neg = [keep.tile([P, S], F32, name=f"neg{t}") for t in range(PACK)]
+        twin = [keep.tile([P, S], F32, name=f"twin{t}") for t in range(PACK)]
+        y = [keep.tile([P, PACK, hi - lo], F32, name=f"y{c}") for c, (lo, hi) in enumerate(CHUNKS)]
+        yb = [keep.tile([P, hi - lo, PACK], BF16, name=f"yb{c}", align_bytes=64) for c, (lo, hi) in enumerate(CHUNKS)]
+        yq = keep.tile([P, S], I32, name="yq", align_bytes=64)
+        ys = keep.tile([P, S], U8, name="ys", align_bytes=64)
+        out_rows = out_0.rearrange("(p t) j -> p t j", t=PACK)
+        out_words = out_1[0].rearrange("p n t -> p (n t)").bitcast(I32)
+
+        for t in range(PACK):
+            for u in range(2):
+                lo, hi = u * HALF, (u + 1) * HALF
+                nc.scalar.activation(gate[t][:, lo:hi], h2[t][:].indirect(entries(n3_t, lo, hi)), ACT.Sigmoid)
+
+        def gated(t):
+            nc.vector.scalar_tensor_tensor(neg[t][:], h2[t][:], -1.0, gate[t][:], ALU.mult, ALU.mult)
+
+        def hop(t, c):
+            lo, hi = CHUNKS[c]
+            nc.vector.tensor_tensor(
+                y[c][:, t, :], neg[t][:].indirect(entries(n4_t, lo, hi)), twin[t][:, lo:hi], ALU.subtract
+            )
+
+        def interleave(c, copy):
+            copy(
+                yb[c][:].rearrange("p (c i) t -> p c t i", i=4),
+                y[c][:].rearrange("p t (c i) -> p c t i", i=4),
+            )
+
+        def quantise(c):
+            lo, hi = CHUNKS[c]
+            nc.vector.quantize_mx(yq[:, lo:hi].bitcast(FP8X4), ys[:, lo:hi], yb[c][:].rearrange("p c t -> p (c t)"))
+            nc.sync.dma_start(out_words[:, lo:hi], yq[:, lo:hi])
+
+        def store(c):
+            lo, hi = CHUNKS[c]
+            nc.sync.dma_start(out_rows[:, :, lo:hi], y[c][:])
+
+        gated(0)
+        nc.vector.tensor_copy(twin[0][:], neg[0][:])
+        hop(0, 0)
+        gated(1)
+        hop(0, 1)
+        hop(0, 2)
+        gated(2)
+        nc.scalar.copy(twin[2][:], neg[2][:])
+        nc.vector.tensor_copy(twin[1][:], neg[1][:])
+        gated(3)
+        nc.scalar.copy(twin[3][:], neg[3][:])
+        for c in range(3):
+            for t in range(1, PACK):
+                hop(t, c)
+            store(c)
+            if c < 2:
+                interleave(c, nc.scalar.copy)
+        quantise(0)
+        interleave(2, nc.vector.tensor_copy)
+        quantise(1)
+        quantise(2)
+        for q in range(4):
+            queue = nc.sync if q % 2 else nc.scalar
+            queue.dma_start(out_2[0][4 * q : 4 * q + 4, :].bitcast(I32), ys[32 * q : 32 * q + 4, :].bitcast(I32))

@@ -17,7 +17,8 @@ PACK = 4
 T, G, S, W = 1024, 2048, 512, 256
 FLOPS = 2 * 2 * 512 * 512 * 512
 HALF = S // 2
-CHUNKS = ((0, 256), (256, 384), (384, 512))
+Z_SPLIT = 320
+Y_SPLIT = 64
 
 
 def tile_picked_codebondhopg_none_po_kernel(
@@ -58,19 +59,25 @@ def tile_picked_codebondhopg_none_po_kernel(
                 src.rearrange("p (m t) -> p m t", t=PACK),
             )
 
-        xs_win = zeroed_bytes("xs_win", T)
-        ds_win = zeroed_bytes("ds_win", G)
-        nc.scalar.dma_start(xs_win[0:P:8, :].bitcast(I32), x_scales[0].bitcast(I32))
-        nc.scalar.dma_start(ds_win[0:P:8, :].bitcast(I32), d_scales[0].bitcast(I32))
+        def load_scales(name, src, width, queue):
+            tile = keep.tile([P, width], U8, name=name, align_bytes=64)
+            queue.dma_start(tile[:].bitcast(I32), src[0].bitcast(I32).unsqueeze(1).to_broadcast([16, 8, width // 4]))
+            return tile
+
+        def load_words(name, src, width):
+            tile = keep.tile([P, width], I32, name=name)
+            nc.sync.dma_start(tile[:], src[0].rearrange("p n t -> p (n t)").bitcast(I32))
+            return tile
+
+        xs_win = load_scales("xs_win", x_scales, T, nc.scalar)
         offs_t = load_list("offs_t", offs)
         k1_t = load_list("k1_t", k1)
+        ds_win = load_scales("ds_win", d_scales, G, nc.sync)
+        xw_win = load_words("xw_win", x_words, T)
         k2_t = load_list("k2_t", k2)
         n1_t = load_list("n1_t", n1)
+        dw_win = load_words("dw_win", d_words, G)
         n2_t = load_list("n2_t", n2)
-        xw_win = keep.tile([P, T], I32, name="xw_win")
-        nc.sync.dma_start(xw_win[:], x_words[0].rearrange("p n t -> p (n t)").bitcast(I32))
-        dw_win = keep.tile([P, G], I32, name="dw_win")
-        nc.sync.dma_start(dw_win[:], d_words[0].rearrange("p n t -> p (n t)").bitcast(I32))
         n3_t = load_list("n3_t", n3)
         n4_t = load_list("n4_t", n4)
         gs_t = keep.tile([P, PACK], F32, name="gs_t")
@@ -81,39 +88,40 @@ def tile_picked_codebondhopg_none_po_kernel(
         nc.vector.memset(warm[:, 0:1], 0.0)
         nc.scalar.activation(warm[:, 1:2], warm[:, 0:1], ACT.Sigmoid)
 
-        picked1 = keep.tile([P, 2 * S], U8, name="picked1")
+        picked1 = keep.tile([P, 2 * S], U8, name="picked1", tag="picked1")
         nc.vector.tensor_copy(picked1[:, S:], xs_win[:].indirect(offs_t[:]))
         nc.vector.tensor_copy(picked1[:, :S], ds_win[:].indirect(k1_t[:]))
         move_rows(planes1, picked1)
         xq = keep.tile([P, S], I32, name="xq", align_bytes=64)
         nc.vector.tensor_copy(xq[:].bitcast(U32), xw_win[:].bitcast(U32).indirect(offs_t[:]))
-        d1_raw = keep.tile([P, S], I32, name="d1_raw", tag="d1_raw")
+        picked2 = keep.tile([P, S], U8, name="picked2")
+        nc.vector.tensor_copy(picked2[:], ds_win[:].indirect(k2_t[:]))
+        move_rows(planes2, picked2)
+        d1_raw = keep.tile([P, S], I32, name="d1_raw")
         nc.vector.tensor_copy(d1_raw[:].bitcast(U32), dw_win[:].bitcast(U32).indirect(k1_t[:]))
         d1 = keep.tile([P, S], I32, name="d1", align_bytes=64)
         deal_words(d1, d1_raw)
         d1_scale = keep.tile([P, S], U8, name="d1_scale", align_bytes=64)
         deal_bytes(d1_scale[:], planes1[:, :S])
+        d2_raw = keep.tile([P, S], I32, name="d2_raw", tag="picked1")
+        nc.vector.tensor_copy(d2_raw[:].bitcast(U32), dw_win[:].bitcast(U32).indirect(k2_t[:]))
 
-        picked2 = keep.tile([P, S], U8, name="picked2", tag="d1_raw")
-        nc.vector.tensor_copy(picked2[:], ds_win[:].indirect(k2_t[:]))
-        move_rows(planes2, picked2)
-
-        h = []
-        for t in range(PACK):
+        ORDER = (2, 0, 1, 3)
+        h = {}
+        for t in ORDER:
             cols = slice(t * P, (t + 1) * P)
-            acc = psum.tile([P, S], F32, name=f"acc1_{t}")
+            acc = psum.tile([P, S], F32, name=f"acc1_{t}", tag=f"bank{t}")
             nc.tensor.matmul_mx(
                 acc[:], lhsT=d1[:, cols].bitcast(FP8X4), lhsT_scale=d1_scale[:, cols],
                 rhs=xq[:].bitcast(FP8X4), rhs_scale=planes1[:, S:], start=True, stop=True,
             )
-            h_t = keep.tile([P, S], F32, name=f"h{t}")
-            nc.scalar.activation(h_t[:], acc[:], ACT.Copy, scale=0.0625)
-            h.append(h_t)
+            h[t] = keep.tile([P, S], F32, name=f"h{t}")
+            nc.scalar.activation(h[t][:], acc[:], ACT.Copy, scale=0.0625)
 
-        pa = [keep.tile([P, W], F32, name=f"pa{t}", tag=f"pa{t}") for t in range(PACK)]
+        pa = [keep.tile([P, W], F32, name=f"pa{t}", tag=f"pa{t}", align_bytes=64) for t in range(PACK)]
         pb = [keep.tile([P, W], F32, name=f"pb{t}", tag=f"pb{t}", align_bytes=64) for t in range(PACK)]
-        dt = [keep.tile([P, S], F32, name=f"dt{t}") for t in range(PACK)]
-        z = [keep.tile([P, HALF, PACK], BF16, name=f"z{u}", align_bytes=64) for u in range(2)]
+        dt = {}
+        z = keep.tile([P, S, PACK], BF16, name="z", align_bytes=64)
 
         def fetch_a(t):
             nc.vector.tensor_copy(pa[t][:], h[t][:].indirect(n1_t[:]))
@@ -122,117 +130,126 @@ def tile_picked_codebondhopg_none_po_kernel(
             nc.vector.tensor_copy(pb[t][:], h[t][:].indirect(n2_t[:]))
 
         def put_sum(t):
+            dt[t] = keep.tile([P, S], F32, name=f"dt{t}", tag="dt", bufs=3)
             nc.vector.tensor_tensor(dt[t][:].indirect(n1_t[:]), pa[t][:], pb[t][:], ALU.add)
 
         def put_product(t):
             nc.vector.tensor_tensor(dt[t][:].indirect(n2_t[:]), pa[t][:], pb[t][:], ALU.mult)
-            for u in range(2):
-                nc.scalar.activation(
-                    z[u][:, :, t], dt[t][:, u * HALF : (u + 1) * HALF], ACT.Copy, scale=gs_t[:, t : t + 1]
-                )
 
-        fetch_a(0)
-        fetch_b(0)
-        fetch_a(1)
-        put_sum(0)
-        fetch_b(1)
-        put_product(0)
-        fetch_a(2)
-        put_sum(1)
-        fetch_b(2)
-        put_product(1)
-        fetch_a(3)
-        put_sum(2)
-        fetch_b(3)
-        put_product(2)
-        put_sum(3)
-        put_product(3)
+        def weigh(t, hi):
+            nc.scalar.activation(z[:, :hi, t], dt[t][:, :hi], ACT.Copy, scale=gs_t[:, t : t + 1])
 
-        d2_raw = keep.tile([P, S], I32, name="d2_raw", tag="pa3")
-        nc.vector.tensor_copy(d2_raw[:].bitcast(U32), dw_win[:].bitcast(U32).indirect(k2_t[:]))
-        d2_scale = keep.tile([P, S], U8, name="d2_scale", tag="pb3", align_bytes=64)
-        deal_bytes(d2_scale[:], planes2[:])
-        d2 = keep.tile([P, S], I32, name="d2", align_bytes=64)
+        fetch_a(ORDER[0])
+        fetch_b(ORDER[0])
+        for t, nxt in zip(ORDER, ORDER[1:]):
+            fetch_a(nxt)
+            put_sum(t)
+            fetch_b(nxt)
+            put_product(t)
+            weigh(t, S)
+        last = ORDER[-1]
+        put_sum(last)
+        d2 = keep.tile([P, S], I32, name="d2", tag=f"pa{ORDER[-2]}", align_bytes=64)
         deal_words(d2, d2_raw)
+        put_product(last)
+        weigh(last, Z_SPLIT)
+
+        nc.vector.tensor_scalar(z[:, Z_SPLIT:, last], dt[last][:, Z_SPLIT:], gs_t[:, last : last + 1], None, ALU.mult)
+        d2_scale = keep.tile([P, S], U8, name="d2_scale", tag=f"pb{last}", align_bytes=64)
+        deal_bytes(d2_scale[:], planes2[:])
         zq = keep.tile([P, S], I32, name="zq", align_bytes=64)
         zs = keep.tile([P, S], U8, name="zs", align_bytes=64)
-        for u in range(2):
-            cols = slice(u * HALF, (u + 1) * HALF)
-            nc.vector.quantize_mx(zq[:, cols].bitcast(FP8X4), zs[:, cols], z[u][:].rearrange("p c t -> p (c t)"))
+        halves = [slice(0, HALF), slice(HALF, S)]
+        for half in halves:
+            nc.vector.quantize_mx(zq[:, half].bitcast(FP8X4), zs[:, half], z[:, half, :].rearrange("p c t -> p (c t)"))
 
-        h2 = [keep.tile([P, S], F32, name=f"h2_{t}") for t in range(PACK)]
-        for t in range(PACK):
+        def second(t, lo, hi, bank):
             cols = slice(t * P, (t + 1) * P)
-            acc = psum.tile([P, S], F32, name=f"acc2_{t}")
+            acc = psum.tile([P, hi - lo], F32, name=f"acc2_{bank}", tag=f"bank{bank}")
             nc.tensor.matmul_mx(
                 acc[:], lhsT=d2[:, cols].bitcast(FP8X4), lhsT_scale=d2_scale[:, cols],
-                rhs=zq[:].bitcast(FP8X4), rhs_scale=zs[:], start=True, stop=True,
+                rhs=zq[:, lo:hi].bitcast(FP8X4), rhs_scale=zs[:, lo:hi], start=True, stop=True,
             )
-            if t == 0:
-                nc.scalar.activation(h2[t][:], acc[:], ACT.Copy, scale=0.0625)
-            else:
-                nc.vector.tensor_scalar(h2[t][:], acc[:], 0.0625, None, ALU.mult)
+            return acc
 
+        h2 = [keep.tile([P, S], F32, name=f"h2_{t}") for t in range(PACK)]
         gate = [keep.tile([P, S], F32, name=f"gate{t}") for t in range(PACK)]
         neg = [keep.tile([P, S], F32, name=f"neg{t}") for t in range(PACK)]
-        twin = [keep.tile([P, S], F32, name=f"twin{t}") for t in range(PACK)]
-        y = [keep.tile([P, PACK, hi - lo], F32, name=f"y{c}") for c, (lo, hi) in enumerate(CHUNKS)]
-        yb = [keep.tile([P, hi - lo, PACK], BF16, name=f"yb{c}", align_bytes=64) for c, (lo, hi) in enumerate(CHUNKS)]
+        twin = {}
+        y = [keep.tile([P, PACK, HALF], F32, name=f"y{u}") for u in range(2)]
+        yb = [keep.tile([P, HALF, PACK], BF16, name=f"yb{u}", align_bytes=64) for u in range(2)]
         yq = keep.tile([P, S], I32, name="yq", align_bytes=64)
         ys = keep.tile([P, S], U8, name="ys", align_bytes=64)
         out_rows = out_0.rearrange("(p t) j -> p t j", t=PACK)
         out_words = out_1[0].rearrange("p n t -> p (n t)").bitcast(I32)
 
-        for t in range(PACK):
+        def half_of(lst, u):
+            return entries(lst, u * HALF, (u + 1) * HALF)
+
+        acc_a = second(0, 0, HALF, 4)
+        acc_b = second(0, HALF, S, 5)
+        for half, acc in zip(halves, (acc_a, acc_b)):
+            nc.scalar.activation(gate[0][:, half], acc[:], ACT.Sigmoid, scale=0.0625)
+            nc.vector.tensor_scalar(h2[0][:, half], acc[:], -0.0625, None, ALU.mult)
+        for u in range(2):
+            nc.vector.tensor_tensor(neg[0][:, halves[u]], gate[0][:].indirect(half_of(n3_t, u)), h2[0][:, halves[u]], ALU.mult)
+        for t in range(1, PACK):
+            acc = second(t, 0, S, t)
+            nc.scalar.activation(h2[t][:], acc[:], ACT.Copy, scale=0.0625)
             for u in range(2):
-                lo, hi = u * HALF, (u + 1) * HALF
-                nc.scalar.activation(gate[t][:, lo:hi], h2[t][:].indirect(entries(n3_t, lo, hi)), ACT.Sigmoid)
+                nc.scalar.activation(gate[t][:, halves[u]], h2[t][:].indirect(half_of(n3_t, u)), ACT.Sigmoid)
 
         def gated(t):
             nc.vector.scalar_tensor_tensor(neg[t][:], h2[t][:], -1.0, gate[t][:], ALU.mult, ALU.mult)
 
-        def hop(t, c):
-            lo, hi = CHUNKS[c]
-            nc.vector.tensor_tensor(
-                y[c][:, t, :], neg[t][:].indirect(entries(n4_t, lo, hi)), twin[t][:, lo:hi], ALU.subtract
-            )
+        def hop(t, u):
+            nc.vector.tensor_tensor(y[u][:, t, :], neg[t][:].indirect(half_of(n4_t, u)), twin[t, u][:], ALU.subtract)
 
-        def interleave(c, copy):
+        def interleave(u, lo, hi, copy):
             copy(
-                yb[c][:].rearrange("p (c i) t -> p c t i", i=4),
-                y[c][:].rearrange("p t (c i) -> p c t i", i=4),
+                yb[u][:, lo:hi, :].rearrange("p (c i) t -> p c t i", i=4),
+                y[u][:, :, lo:hi].rearrange("p t (c i) -> p c t i", i=4),
             )
 
-        def quantise(c):
-            lo, hi = CHUNKS[c]
-            nc.vector.quantize_mx(yq[:, lo:hi].bitcast(FP8X4), ys[:, lo:hi], yb[c][:].rearrange("p c t -> p (c t)"))
-            nc.sync.dma_start(out_words[:, lo:hi], yq[:, lo:hi])
+        def quantise(u):
+            nc.vector.quantize_mx(yq[:, halves[u]].bitcast(FP8X4), ys[:, halves[u]], yb[u][:].rearrange("p c t -> p (c t)"))
+            nc.sync.dma_start(out_words[:, halves[u]], yq[:, halves[u]])
 
-        def store(c):
-            lo, hi = CHUNKS[c]
-            nc.sync.dma_start(out_rows[:, :, lo:hi], y[c][:])
+        def store(u, t0):
+            nc.sync.dma_start(out_rows[:, t0 : t0 + 2, halves[u]], y[u][:, t0 : t0 + 2, :])
 
-        gated(0)
-        nc.vector.tensor_copy(twin[0][:], neg[0][:])
+        def duplicate(t, u, copy, tag):
+            twin[t, u] = keep.tile([P, HALF], F32, name=f"twin{t}_{u}", tag=tag)
+            copy(twin[t, u][:], neg[t][:, halves[u]])
+
+        duplicate(0, 0, nc.vector.tensor_copy, "twin00")
+        duplicate(0, 1, nc.vector.tensor_copy, "twin01")
         hop(0, 0)
         gated(1)
         hop(0, 1)
-        hop(0, 2)
+        duplicate(1, 0, nc.vector.tensor_copy, "twin10")
+        duplicate(1, 1, nc.vector.tensor_copy, "twin11")
         gated(2)
-        nc.scalar.copy(twin[2][:], neg[2][:])
-        nc.vector.tensor_copy(twin[1][:], neg[1][:])
+        duplicate(2, 0, nc.scalar.copy, "twin20")
+        hop(1, 0)
+        store(0, 0)
+        hop(1, 1)
+        store(1, 0)
         gated(3)
-        nc.scalar.copy(twin[3][:], neg[3][:])
-        for c in range(3):
-            for t in range(1, PACK):
-                hop(t, c)
-            store(c)
-            if c < 2:
-                interleave(c, nc.scalar.copy)
+        duplicate(3, 0, nc.scalar.copy, "twin30")
+        duplicate(2, 1, nc.scalar.copy, "gate3")
+        duplicate(3, 1, nc.scalar.copy, "twin31")
+        hop(2, 0)
+        hop(3, 0)
+        store(0, 2)
+        interleave(0, 0, HALF, nc.scalar.copy)
+        hop(2, 1)
+        hop(3, 1)
+        store(1, 2)
+        interleave(1, 0, Y_SPLIT, nc.scalar.copy)
+        interleave(1, Y_SPLIT, HALF, nc.vector.tensor_copy)
         quantise(0)
-        interleave(2, nc.vector.tensor_copy)
         quantise(1)
-        quantise(2)
         for q in range(4):
             queue = nc.sync if q % 2 else nc.scalar
             queue.dma_start(out_2[0][4 * q : 4 * q + 4, :].bitcast(I32), ys[32 * q : 32 * q + 4, :].bitcast(I32))

@@ -17,8 +17,8 @@ PACK = 4
 T, G, S, W = 1024, 2048, 512, 256
 FLOPS = 2 * 2 * 512 * 512 * 512
 HALF = S // 2
-Z_SPLIT = 320
-Y_SPLIT = 64
+Z_SPLIT = 224
+Y_SPLIT = 96
 
 
 def tile_picked_codebondhopg_none_po_kernel(
@@ -53,10 +53,10 @@ def tile_picked_codebondhopg_none_po_kernel(
                 src[:].bitcast(U32).rearrange("p (c i t) -> p c t i", t=PACK, i=4),
             )
 
-        def deal_bytes(dst, src):
+        def deal_bytes(dst, src, t0, t1):
             nc.vector.tensor_copy(
-                dst.rearrange("p (t m) -> p m t", t=PACK),
-                src.rearrange("p (m t) -> p m t", t=PACK),
+                dst.rearrange("p (t m) -> p t m", t=PACK)[:, t0:t1, :],
+                src.rearrange("p (m t) -> p t m", t=PACK)[:, t0:t1, :],
             )
 
         def load_scales(name, src, width, queue):
@@ -102,11 +102,12 @@ def tile_picked_codebondhopg_none_po_kernel(
         d1 = keep.tile([P, S], I32, name="d1", align_bytes=64)
         deal_words(d1, d1_raw)
         d1_scale = keep.tile([P, S], U8, name="d1_scale", align_bytes=64)
-        deal_bytes(d1_scale[:], planes1[:, :S])
+        deal_bytes(d1_scale[:], planes1[:, :S], 0, 1)
+        deal_bytes(d1_scale[:], planes1[:, :S], 1, PACK)
         d2_raw = keep.tile([P, S], I32, name="d2_raw", tag="picked1")
         nc.vector.tensor_copy(d2_raw[:].bitcast(U32), dw_win[:].bitcast(U32).indirect(k2_t[:]))
 
-        ORDER = (2, 0, 1, 3)
+        ORDER = (0, 2, 3, 1)
         h = {}
         for t in ORDER:
             cols = slice(t * P, (t + 1) * P)
@@ -156,12 +157,13 @@ def tile_picked_codebondhopg_none_po_kernel(
 
         nc.vector.tensor_scalar(z[:, Z_SPLIT:, last], dt[last][:, Z_SPLIT:], gs_t[:, last : last + 1], None, ALU.mult)
         d2_scale = keep.tile([P, S], U8, name="d2_scale", tag=f"pb{last}", align_bytes=64)
-        deal_bytes(d2_scale[:], planes2[:])
+        deal_bytes(d2_scale[:], planes2[:], 0, 1)
         zq = keep.tile([P, S], I32, name="zq", align_bytes=64)
         zs = keep.tile([P, S], U8, name="zs", align_bytes=64)
         halves = [slice(0, HALF), slice(HALF, S)]
         for half in halves:
             nc.vector.quantize_mx(zq[:, half].bitcast(FP8X4), zs[:, half], z[:, half, :].rearrange("p c t -> p (c t)"))
+        deal_bytes(d2_scale[:], planes2[:], 1, PACK)
 
         def second(t, lo, hi, bank):
             cols = slice(t * P, (t + 1) * P)

@@ -14,17 +14,27 @@ ACT = mybir.ActivationFunctionType
 
 P = 128
 PACK = 4
-T, G, S, W = 1024, 2048, 512, 256
-FLOPS = 2 * 2 * 512 * 512 * 512
+QUADRANT = 32
+BLOCK_ROWS = 8
+LINE = 4
+LIST_ROWS = 16
+TOKENS, CODEWORDS = 1024, 2048
+S = 512
 HALF = S // 2
+SIXTEENTH = 0.0625
+FLOPS = 2 * 2 * S * S * S
+
+PAIR_ORDER = (0, 2, 3, 1)
+DT_BUFFERS = PACK - 1
 Z_SPLIT = 224
-Y_SPLIT = 96
+Y_SPLIT = 80
 
 
 def tile_picked_codebondhopg_none_po_kernel(
     tc, x_words, x_scales, d_words, d_scales, gs, offs, k1, n1, n2, k2, n3, n4, out_0, out_1, out_2
 ):
     nc = tc.nc
+    halves = [slice(0, HALF), slice(HALF, S)]
     with ExitStack() as ctx:
         keep = ctx.enter_context(tc.tile_pool(name="keep", bufs=1))
         psum = ctx.enter_context(tc.psum_pool(name="psum", bufs=1))
@@ -34,34 +44,13 @@ def tile_picked_codebondhopg_none_po_kernel(
             nc.sync.dma_start(tile[:], src)
             return tile
 
-        def entries(lst, lo, hi):
-            return lst[:, lo // 16 : hi // 16]
-
-        def zeroed_bytes(name, width):
-            tile = keep.tile([P, width], U8, name=name, align_bytes=64)
-            nc.vector.memset(tile[:].bitcast(I32), 0)
-            return tile
-
-        def move_rows(dst, src):
-            for j in range(4):
-                queue = nc.sync if j % 2 else nc.scalar
-                queue.dma_start(dst[j:P:32, :].bitcast(I32), src[8 * j : P : 32, :].bitcast(I32))
-
-        def deal_words(dst, src):
-            nc.vector.tensor_copy(
-                dst[:].bitcast(U32).rearrange("p (t c i) -> p c t i", t=PACK, i=4),
-                src[:].bitcast(U32).rearrange("p (c i t) -> p c t i", t=PACK, i=4),
-            )
-
-        def deal_bytes(dst, src, t0, t1):
-            nc.vector.tensor_copy(
-                dst.rearrange("p (t m) -> p t m", t=PACK)[:, t0:t1, :],
-                src.rearrange("p (m t) -> p t m", t=PACK)[:, t0:t1, :],
-            )
+        def half_of(list_tile, u):
+            return list_tile[:, u * HALF // LIST_ROWS : (u + 1) * HALF // LIST_ROWS]
 
         def load_scales(name, src, width, queue):
             tile = keep.tile([P, width], U8, name=name, align_bytes=64)
-            queue.dma_start(tile[:].bitcast(I32), src[0].bitcast(I32).unsqueeze(1).to_broadcast([16, 8, width // 4]))
+            rows = src[0].bitcast(I32).unsqueeze(1).to_broadcast([P // BLOCK_ROWS, BLOCK_ROWS, width // 4])
+            queue.dma_start(tile[:].bitcast(I32), rows)
             return tile
 
         def load_words(name, src, width):
@@ -69,189 +58,234 @@ def tile_picked_codebondhopg_none_po_kernel(
             nc.sync.dma_start(tile[:], src[0].rearrange("p n t -> p (n t)").bitcast(I32))
             return tile
 
-        xs_win = load_scales("xs_win", x_scales, T, nc.scalar)
-        offs_t = load_list("offs_t", offs)
-        k1_t = load_list("k1_t", k1)
-        ds_win = load_scales("ds_win", d_scales, G, nc.sync)
-        xw_win = load_words("xw_win", x_words, T)
-        k2_t = load_list("k2_t", k2)
-        n1_t = load_list("n1_t", n1)
-        dw_win = load_words("dw_win", d_words, G)
-        n2_t = load_list("n2_t", n2)
-        n3_t = load_list("n3_t", n3)
-        n4_t = load_list("n4_t", n4)
-        gs_t = keep.tile([P, PACK], F32, name="gs_t")
-        nc.gpsimd.dma_start(gs_t[:], gs.rearrange("(p t) o -> p (t o)", t=PACK))
-        planes1 = zeroed_bytes("planes1", 2 * S)
-        planes2 = zeroed_bytes("planes2", S)
+        def zeroed_bytes(name, width):
+            tile = keep.tile([P, width], U8, name=name, align_bytes=64)
+            nc.vector.memset(tile[:].bitcast(I32), 0)
+            return tile
+
+        def place_scale_rows(dst, src):
+            for j in range(QUADRANT // BLOCK_ROWS):
+                queue = nc.sync if j % 2 else nc.scalar
+                queue.dma_start(dst[j:P:QUADRANT, :].bitcast(I32), src[BLOCK_ROWS * j : P : QUADRANT, :].bitcast(I32))
+
+        def gather_words(dst, window, list_tile):
+            nc.vector.tensor_copy(dst[:].bitcast(U32), window[:].bitcast(U32).indirect(list_tile[:]))
+
+        def deal_words(dst, src):
+            nc.vector.tensor_copy(
+                dst[:].bitcast(U32).rearrange("p (t c i) -> p c t i", t=PACK, i=LINE),
+                src[:].bitcast(U32).rearrange("p (c i t) -> p c t i", t=PACK, i=LINE),
+            )
+
+        def deal_bytes(dst, src, row_tiles):
+            nc.vector.tensor_copy(
+                dst.rearrange("p (t m) -> p t m", t=PACK)[:, row_tiles, :],
+                src.rearrange("p (m t) -> p t m", t=PACK)[:, row_tiles, :],
+            )
+
+        def product(bank, codes, scales, t, moving, moving_scales):
+            columns = slice(t * P, (t + 1) * P)
+            acc = psum.tile([P, moving.shape[1]], F32, name=f"acc_{bank}", tag=f"bank{bank}")
+            nc.tensor.matmul_mx(
+                acc[:],
+                lhsT=codes[:, columns].bitcast(FP8X4),
+                lhsT_scale=scales[:, columns],
+                rhs=moving.bitcast(FP8X4),
+                rhs_scale=moving_scales,
+                start=True,
+                stop=True,
+            )
+            return acc
+
+        first_tile, other_tiles = slice(0, 1), slice(1, PACK)
+
+        x_scale_table = load_scales("x_scale_table", x_scales, TOKENS, nc.scalar)
+        offs_list = load_list("offs_list", offs)
+        k1_list = load_list("k1_list", k1)
+        d_scale_table = load_scales("d_scale_table", d_scales, CODEWORDS, nc.sync)
+        x_word_table = load_words("x_word_table", x_words, TOKENS)
+        k2_list = load_list("k2_list", k2)
+        n1_list = load_list("n1_list", n1)
+        d_word_table = load_words("d_word_table", d_words, CODEWORDS)
+        n2_list = load_list("n2_list", n2)
+        n3_list = load_list("n3_list", n3)
+        n4_list = load_list("n4_list", n4)
+        gains = keep.tile([P, PACK], F32, name="gains")
+        nc.gpsimd.dma_start(gains[:], gs.rearrange("(p t) o -> p (t o)", t=PACK))
+        placed1 = zeroed_bytes("placed1", 2 * S)
+        placed2 = zeroed_bytes("placed2", S)
         warm = keep.tile([P, 2], F32, name="warm")
         nc.vector.memset(warm[:, 0:1], 0.0)
         nc.scalar.activation(warm[:, 1:2], warm[:, 0:1], ACT.Sigmoid)
 
         picked1 = keep.tile([P, 2 * S], U8, name="picked1", tag="picked1")
-        nc.vector.tensor_copy(picked1[:, S:], xs_win[:].indirect(offs_t[:]))
-        nc.vector.tensor_copy(picked1[:, :S], ds_win[:].indirect(k1_t[:]))
-        move_rows(planes1, picked1)
-        xq = keep.tile([P, S], I32, name="xq", align_bytes=64)
-        nc.vector.tensor_copy(xq[:].bitcast(U32), xw_win[:].bitcast(U32).indirect(offs_t[:]))
+        nc.vector.tensor_copy(picked1[:, S:], x_scale_table[:].indirect(offs_list[:]))
+        nc.vector.tensor_copy(picked1[:, :S], d_scale_table[:].indirect(k1_list[:]))
+        place_scale_rows(placed1, picked1)
+        x_codes = keep.tile([P, S], I32, name="x_codes", align_bytes=64)
+        gather_words(x_codes, x_word_table, offs_list)
         picked2 = keep.tile([P, S], U8, name="picked2")
-        nc.vector.tensor_copy(picked2[:], ds_win[:].indirect(k2_t[:]))
-        move_rows(planes2, picked2)
-        d1_raw = keep.tile([P, S], I32, name="d1_raw")
-        nc.vector.tensor_copy(d1_raw[:].bitcast(U32), dw_win[:].bitcast(U32).indirect(k1_t[:]))
-        d1 = keep.tile([P, S], I32, name="d1", align_bytes=64)
-        deal_words(d1, d1_raw)
-        d1_scale = keep.tile([P, S], U8, name="d1_scale", align_bytes=64)
-        deal_bytes(d1_scale[:], planes1[:, :S], 0, 1)
-        deal_bytes(d1_scale[:], planes1[:, :S], 1, PACK)
-        d2_raw = keep.tile([P, S], I32, name="d2_raw", tag="picked1")
-        nc.vector.tensor_copy(d2_raw[:].bitcast(U32), dw_win[:].bitcast(U32).indirect(k2_t[:]))
+        nc.vector.tensor_copy(picked2[:], d_scale_table[:].indirect(k2_list[:]))
+        place_scale_rows(placed2, picked2)
+        d1_undealt = keep.tile([P, S], I32, name="d1_undealt")
+        gather_words(d1_undealt, d_word_table, k1_list)
+        d1_scales = keep.tile([P, S], U8, name="d1_scales", align_bytes=64)
+        deal_bytes(d1_scales[:], placed1[:, :S], first_tile)
+        d1_codes = keep.tile([P, S], I32, name="d1_codes", align_bytes=64)
+        deal_words(d1_codes, d1_undealt)
+        deal_bytes(d1_scales[:], placed1[:, :S], other_tiles)
+        d2_undealt = keep.tile([P, S], I32, name="d2_undealt", tag="picked1")
+        gather_words(d2_undealt, d_word_table, k2_list)
 
-        ORDER = (0, 2, 3, 1)
         h = {}
-        for t in ORDER:
-            cols = slice(t * P, (t + 1) * P)
-            acc = psum.tile([P, S], F32, name=f"acc1_{t}", tag=f"bank{t}")
-            nc.tensor.matmul_mx(
-                acc[:], lhsT=d1[:, cols].bitcast(FP8X4), lhsT_scale=d1_scale[:, cols],
-                rhs=xq[:].bitcast(FP8X4), rhs_scale=planes1[:, S:], start=True, stop=True,
-            )
-            h[t] = keep.tile([P, S], F32, name=f"h{t}")
-            nc.scalar.activation(h[t][:], acc[:], ACT.Copy, scale=0.0625)
+        for t in PAIR_ORDER:
+            acc = product(t, d1_codes, d1_scales, t, x_codes[:], placed1[:, S:])
+            h[t] = keep.tile([P, S], F32, name=f"h{t}", tag=f"h{t}", align_bytes=64)
+            nc.scalar.activation(h[t][:], acc[:], ACT.Copy, scale=SIXTEENTH)
 
-        pa = [keep.tile([P, W], F32, name=f"pa{t}", tag=f"pa{t}", align_bytes=64) for t in range(PACK)]
-        pb = [keep.tile([P, W], F32, name=f"pb{t}", tag=f"pb{t}", align_bytes=64) for t in range(PACK)]
+        last = PAIR_ORDER[-1]
+        h2_windows = {t: keep.tile([P, 2 * S], F32, name=f"h2_window{t}") for t in range(1, PACK)}
+        pairs = {t: h2_windows[owner][:, S:] for t, owner in zip(PAIR_ORDER[:-1], range(1, PACK))}
+        last_pair = keep.tile([P, S], F32, name="last_pair", tag="last_pair", align_bytes=64)
+        pairs[last] = last_pair[:]
+        pa = {t: pairs[t][:, halves[0]] for t in PAIR_ORDER}
+        pb = {t: pairs[t][:, halves[1]] for t in PAIR_ORDER}
         dt = {}
         z = keep.tile([P, S, PACK], BF16, name="z", align_bytes=64)
 
-        def fetch_a(t):
-            nc.vector.tensor_copy(pa[t][:], h[t][:].indirect(n1_t[:]))
-
-        def fetch_b(t):
-            nc.vector.tensor_copy(pb[t][:], h[t][:].indirect(n2_t[:]))
+        def fetch(dst, t, list_tile):
+            nc.vector.tensor_copy(dst[t], h[t][:].indirect(list_tile[:]))
 
         def put_sum(t):
-            dt[t] = keep.tile([P, S], F32, name=f"dt{t}", tag="dt", bufs=3)
-            nc.vector.tensor_tensor(dt[t][:].indirect(n1_t[:]), pa[t][:], pb[t][:], ALU.add)
+            dt[t] = keep.tile([P, S], F32, name=f"dt{t}", tag="dt", bufs=DT_BUFFERS)
+            nc.vector.tensor_tensor(dt[t][:].indirect(n1_list[:]), pa[t], pb[t], ALU.add)
 
         def put_product(t):
-            nc.vector.tensor_tensor(dt[t][:].indirect(n2_t[:]), pa[t][:], pb[t][:], ALU.mult)
+            nc.vector.tensor_tensor(dt[t][:].indirect(n2_list[:]), pa[t], pb[t], ALU.mult)
 
-        def weigh(t, hi):
-            nc.scalar.activation(z[:, :hi, t], dt[t][:, :hi], ACT.Copy, scale=gs_t[:, t : t + 1])
+        def weigh(t, columns):
+            nc.scalar.activation(z[:, columns, t], dt[t][:, columns], ACT.Copy, scale=gains[:, t : t + 1])
 
-        fetch_a(ORDER[0])
-        fetch_b(ORDER[0])
-        for t, nxt in zip(ORDER, ORDER[1:]):
-            fetch_a(nxt)
+        fetch(pa, PAIR_ORDER[0], n1_list)
+        fetch(pb, PAIR_ORDER[0], n2_list)
+        for t, following in zip(PAIR_ORDER, PAIR_ORDER[1:]):
+            fetch(pa, following, n1_list)
             put_sum(t)
-            fetch_b(nxt)
+            fetch(pb, following, n2_list)
             put_product(t)
-            weigh(t, S)
-        last = ORDER[-1]
+            weigh(t, slice(0, S))
         put_sum(last)
-        d2 = keep.tile([P, S], I32, name="d2", tag=f"pa{ORDER[-2]}", align_bytes=64)
-        deal_words(d2, d2_raw)
+        d2_codes = keep.tile([P, S], I32, name="d2_codes", tag=f"h{last}", align_bytes=64)
+        deal_words(d2_codes, d2_undealt)
         put_product(last)
-        weigh(last, Z_SPLIT)
+        weigh(last, slice(0, Z_SPLIT))
+        nc.vector.tensor_scalar(z[:, Z_SPLIT:, last], dt[last][:, Z_SPLIT:], gains[:, last : last + 1], None, ALU.mult)
 
-        nc.vector.tensor_scalar(z[:, Z_SPLIT:, last], dt[last][:, Z_SPLIT:], gs_t[:, last : last + 1], None, ALU.mult)
-        d2_scale = keep.tile([P, S], U8, name="d2_scale", tag=f"pb{last}", align_bytes=64)
-        deal_bytes(d2_scale[:], planes2[:], 0, 1)
-        zq = keep.tile([P, S], I32, name="zq", align_bytes=64)
-        zs = keep.tile([P, S], U8, name="zs", align_bytes=64)
-        halves = [slice(0, HALF), slice(HALF, S)]
+        d2_scales = keep.tile([P, S], U8, name="d2_scales", tag="last_pair", align_bytes=64)
+        deal_bytes(d2_scales[:], placed2[:], first_tile)
+        z_codes = keep.tile([P, S], I32, name="z_codes", align_bytes=64)
+        z_scales = keep.tile([P, S], U8, name="z_scales", align_bytes=64)
         for half in halves:
-            nc.vector.quantize_mx(zq[:, half].bitcast(FP8X4), zs[:, half], z[:, half, :].rearrange("p c t -> p (c t)"))
-        deal_bytes(d2_scale[:], planes2[:], 1, PACK)
-
-        def second(t, lo, hi, bank):
-            cols = slice(t * P, (t + 1) * P)
-            acc = psum.tile([P, hi - lo], F32, name=f"acc2_{bank}", tag=f"bank{bank}")
-            nc.tensor.matmul_mx(
-                acc[:], lhsT=d2[:, cols].bitcast(FP8X4), lhsT_scale=d2_scale[:, cols],
-                rhs=zq[:, lo:hi].bitcast(FP8X4), rhs_scale=zs[:, lo:hi], start=True, stop=True,
+            nc.vector.quantize_mx(
+                z_codes[:, half].bitcast(FP8X4), z_scales[:, half], z[:, half, :].rearrange("p c t -> p (c t)")
             )
-            return acc
+        deal_bytes(d2_scales[:], placed2[:], other_tiles)
 
-        h2 = [keep.tile([P, S], F32, name=f"h2_{t}") for t in range(PACK)]
-        gate = [keep.tile([P, S], F32, name=f"gate{t}") for t in range(PACK)]
-        neg = [keep.tile([P, S], F32, name=f"neg{t}") for t in range(PACK)]
+        neg_st = [keep.tile([P, S], F32, name=f"neg_st{t}") for t in range(PACK)]
+
+        sigmoid0 = keep.tile([P, S], F32, name="sigmoid0")
+        neg_h2_0 = keep.tile([P, S], F32, name="neg_h2_0")
+        half_accs = [
+            product(PACK + u, d2_codes, d2_scales, 0, z_codes[:, half], z_scales[:, half])
+            for u, half in enumerate(halves)
+        ]
+        for half, acc in zip(halves, half_accs):
+            nc.scalar.activation(sigmoid0[:, half], acc[:], ACT.Sigmoid, scale=SIXTEENTH)
+            nc.vector.tensor_scalar(neg_h2_0[:, half], acc[:], -SIXTEENTH, None, ALU.mult)
+        for u, half in enumerate(halves):
+            nc.vector.tensor_tensor(
+                neg_st[0][:, half], sigmoid0[:].indirect(half_of(n3_list, u)), neg_h2_0[:, half], ALU.mult
+            )
+
+        gate = {t: keep.tile([P, S], F32, name=f"gate{t}", tag=f"gate{t}") for t in range(1, PACK)}
+
+        def leave_bank(t):
+            acc = product(t, d2_codes, d2_scales, t, z_codes[:], z_scales[:])
+            nc.scalar.activation(h2_windows[t][:, :S], acc[:], ACT.Copy, scale=SIXTEENTH)
+
+        leave_bank(1)
+        for t in range(1, PACK):
+            if t + 1 < PACK:
+                leave_bank(t + 1)
+            nc.scalar.activation(gate[t][:], h2_windows[t][:].indirect(n3_list[:]), ACT.Sigmoid)
+
         twin = {}
         y = [keep.tile([P, PACK, HALF], F32, name=f"y{u}") for u in range(2)]
-        yb = [keep.tile([P, HALF, PACK], BF16, name=f"yb{u}", align_bytes=64) for u in range(2)]
-        yq = keep.tile([P, S], I32, name="yq", align_bytes=64)
-        ys = keep.tile([P, S], U8, name="ys", align_bytes=64)
+        y_rounded = [keep.tile([P, HALF, PACK], BF16, name=f"y_rounded{u}", align_bytes=64) for u in range(2)]
+        y_codes = keep.tile([P, S], I32, name="y_codes", align_bytes=64)
+        y_scales = keep.tile([P, S], U8, name="y_scales", align_bytes=64)
         out_rows = out_0.rearrange("(p t) j -> p t j", t=PACK)
         out_words = out_1[0].rearrange("p n t -> p (n t)").bitcast(I32)
 
-        def half_of(lst, u):
-            return entries(lst, u * HALF, (u + 1) * HALF)
+        def apply_gate(t):
+            nc.vector.scalar_tensor_tensor(neg_st[t][:], h2_windows[t][:, :S], -1.0, gate[t][:], ALU.mult, ALU.mult)
 
-        acc_a = second(0, 0, HALF, 4)
-        acc_b = second(0, HALF, S, 5)
-        for half, acc in zip(halves, (acc_a, acc_b)):
-            nc.scalar.activation(gate[0][:, half], acc[:], ACT.Sigmoid, scale=0.0625)
-            nc.vector.tensor_scalar(h2[0][:, half], acc[:], -0.0625, None, ALU.mult)
-        for u in range(2):
-            nc.vector.tensor_tensor(neg[0][:, halves[u]], gate[0][:].indirect(half_of(n3_t, u)), h2[0][:, halves[u]], ALU.mult)
-        for t in range(1, PACK):
-            acc = second(t, 0, S, t)
-            nc.scalar.activation(h2[t][:], acc[:], ACT.Copy, scale=0.0625)
-            for u in range(2):
-                nc.scalar.activation(gate[t][:, halves[u]], h2[t][:].indirect(half_of(n3_t, u)), ACT.Sigmoid)
-
-        def gated(t):
-            nc.vector.scalar_tensor_tensor(neg[t][:], h2[t][:], -1.0, gate[t][:], ALU.mult, ALU.mult)
+        def duplicate(t, u, copy, buffer=None):
+            twin[t, u] = keep.tile([P, HALF], F32, name=f"twin{t}_{u}", tag=buffer or f"twin{t}_{u}")
+            copy(twin[t, u][:], neg_st[t][:, halves[u]])
 
         def hop(t, u):
-            nc.vector.tensor_tensor(y[u][:, t, :], neg[t][:].indirect(half_of(n4_t, u)), twin[t, u][:], ALU.subtract)
+            nc.vector.tensor_tensor(y[u][:, t, :], neg_st[t][:].indirect(half_of(n4_list, u)), twin[t, u][:], ALU.subtract)
 
-        def interleave(u, lo, hi, copy):
+        def store(u, row_tiles):
+            nc.sync.dma_start(out_rows[:, row_tiles, halves[u]], y[u][:, row_tiles, :])
+
+        def round_y(u, columns, copy):
             copy(
-                yb[u][:, lo:hi, :].rearrange("p (c i) t -> p c t i", i=4),
-                y[u][:, :, lo:hi].rearrange("p t (c i) -> p c t i", i=4),
+                y_rounded[u][:, columns, :].rearrange("p (c i) t -> p c t i", i=LINE),
+                y[u][:, :, columns].rearrange("p t (c i) -> p c t i", i=LINE),
             )
 
-        def quantise(u):
-            nc.vector.quantize_mx(yq[:, halves[u]].bitcast(FP8X4), ys[:, halves[u]], yb[u][:].rearrange("p c t -> p (c t)"))
-            nc.sync.dma_start(out_words[:, halves[u]], yq[:, halves[u]])
+        def quantise_y(u):
+            half = halves[u]
+            nc.vector.quantize_mx(
+                y_codes[:, half].bitcast(FP8X4), y_scales[:, half], y_rounded[u][:].rearrange("p c t -> p (c t)")
+            )
+            nc.sync.dma_start(out_words[:, half], y_codes[:, half])
 
-        def store(u, t0):
-            nc.sync.dma_start(out_rows[:, t0 : t0 + 2, halves[u]], y[u][:, t0 : t0 + 2, :])
-
-        def duplicate(t, u, copy, tag):
-            twin[t, u] = keep.tile([P, HALF], F32, name=f"twin{t}_{u}", tag=tag)
-            copy(twin[t, u][:], neg[t][:, halves[u]])
-
-        duplicate(0, 0, nc.vector.tensor_copy, "twin00")
-        duplicate(0, 1, nc.vector.tensor_copy, "twin01")
+        low_tiles, high_tiles = slice(0, 2), slice(2, PACK)
+        duplicate(0, 0, nc.vector.tensor_copy)
+        duplicate(0, 1, nc.vector.tensor_copy)
         hop(0, 0)
-        gated(1)
+        apply_gate(1)
         hop(0, 1)
-        duplicate(1, 0, nc.vector.tensor_copy, "twin10")
-        duplicate(1, 1, nc.vector.tensor_copy, "twin11")
-        gated(2)
-        duplicate(2, 0, nc.scalar.copy, "twin20")
+        duplicate(1, 0, nc.vector.tensor_copy)
+        apply_gate(2)
+        duplicate(2, 0, nc.scalar.copy)
+        duplicate(1, 1, nc.scalar.copy)
         hop(1, 0)
-        store(0, 0)
-        hop(1, 1)
-        store(1, 0)
-        gated(3)
-        duplicate(3, 0, nc.scalar.copy, "twin30")
-        duplicate(2, 1, nc.scalar.copy, "gate3")
-        duplicate(3, 1, nc.scalar.copy, "twin31")
+        store(0, low_tiles)
+        apply_gate(3)
+        duplicate(3, 0, nc.scalar.copy)
+        duplicate(2, 1, nc.scalar.copy, buffer="gate3")
+        duplicate(3, 1, nc.scalar.copy)
         hop(2, 0)
+        hop(1, 1)
+        store(1, low_tiles)
         hop(3, 0)
-        store(0, 2)
-        interleave(0, 0, HALF, nc.scalar.copy)
+        store(0, high_tiles)
+        round_y(0, slice(0, HALF), nc.scalar.copy)
         hop(2, 1)
         hop(3, 1)
-        store(1, 2)
-        interleave(1, 0, Y_SPLIT, nc.scalar.copy)
-        interleave(1, Y_SPLIT, HALF, nc.vector.tensor_copy)
-        quantise(0)
-        quantise(1)
-        for q in range(4):
+        store(1, high_tiles)
+        round_y(1, slice(0, Y_SPLIT), nc.scalar.copy)
+        round_y(1, slice(Y_SPLIT, HALF), nc.vector.tensor_copy)
+        quantise_y(0)
+        quantise_y(1)
+
+        for q in range(P // QUADRANT):
             queue = nc.sync if q % 2 else nc.scalar
-            queue.dma_start(out_2[0][4 * q : 4 * q + 4, :].bitcast(I32), ys[32 * q : 32 * q + 4, :].bitcast(I32))
+            queue.dma_start(
+                out_2[0][PACK * q : PACK * (q + 1), :].bitcast(I32),
+                y_scales[QUADRANT * q : QUADRANT * q + PACK, :].bitcast(I32),
+            )

from contextlib import ExitStack

import concourse.mybir as mybir

F32 = mybir.dt.float32
BF16 = mybir.dt.bfloat16
I32 = mybir.dt.int32
U32 = mybir.dt.uint32
U16 = mybir.dt.uint16
U8 = mybir.dt.uint8
FP8X4 = mybir.dt.float8_e4m3fn_x4
ALU = mybir.AluOpType
ACT = mybir.ActivationFunctionType

P = 128
PACK = 4
QUADRANT = 32
BLOCK_ROWS = 8
LINE = 4
LIST_ROWS = 16
TOKENS, CODEWORDS = 1024, 2048
S = 512
HALF = S // 2
SIXTEENTH = 0.0625
FLOPS = 2 * 2 * S * S * S

PAIR_ORDER = (0, 2, 3, 1)
DT_BUFFERS = PACK - 1
Z_SPLIT = 224
Y_SPLIT = 80


def tile_picked_codebondhopg_none_po_kernel(
    tc, x_words, x_scales, d_words, d_scales, gs, offs, k1, n1, n2, k2, n3, n4, out_0, out_1, out_2
):
    nc = tc.nc
    halves = [slice(0, HALF), slice(HALF, S)]
    with ExitStack() as ctx:
        keep = ctx.enter_context(tc.tile_pool(name="keep", bufs=1))
        psum = ctx.enter_context(tc.psum_pool(name="psum", bufs=1))

        def load_list(name, src):
            tile = keep.tile(list(src.shape), U16, name=name)
            nc.sync.dma_start(tile[:], src)
            return tile

        def half_of(list_tile, u):
            return list_tile[:, u * HALF // LIST_ROWS : (u + 1) * HALF // LIST_ROWS]

        def load_scales(name, src, width, queue):
            tile = keep.tile([P, width], U8, name=name, align_bytes=64)
            rows = src[0].bitcast(I32).unsqueeze(1).to_broadcast([P // BLOCK_ROWS, BLOCK_ROWS, width // 4])
            queue.dma_start(tile[:].bitcast(I32), rows)
            return tile

        def load_words(name, src, width):
            tile = keep.tile([P, width], I32, name=name)
            nc.sync.dma_start(tile[:], src[0].rearrange("p n t -> p (n t)").bitcast(I32))
            return tile

        def zeroed_bytes(name, width):
            tile = keep.tile([P, width], U8, name=name, align_bytes=64)
            nc.vector.memset(tile[:].bitcast(I32), 0)
            return tile

        def place_scale_rows(dst, src):
            for j in range(QUADRANT // BLOCK_ROWS):
                queue = nc.sync if j % 2 else nc.scalar
                queue.dma_start(dst[j:P:QUADRANT, :].bitcast(I32), src[BLOCK_ROWS * j : P : QUADRANT, :].bitcast(I32))

        def gather_words(dst, window, list_tile):
            nc.vector.tensor_copy(dst[:].bitcast(U32), window[:].bitcast(U32).indirect(list_tile[:]))

        def deal_words(dst, src):
            nc.vector.tensor_copy(
                dst[:].bitcast(U32).rearrange("p (t c i) -> p c t i", t=PACK, i=LINE),
                src[:].bitcast(U32).rearrange("p (c i t) -> p c t i", t=PACK, i=LINE),
            )

        def deal_bytes(dst, src, row_tiles):
            nc.vector.tensor_copy(
                dst.rearrange("p (t m) -> p t m", t=PACK)[:, row_tiles, :],
                src.rearrange("p (m t) -> p t m", t=PACK)[:, row_tiles, :],
            )

        def product(bank, codes, scales, t, moving, moving_scales):
            columns = slice(t * P, (t + 1) * P)
            acc = psum.tile([P, moving.shape[1]], F32, name=f"acc_{bank}", tag=f"bank{bank}")
            nc.tensor.matmul_mx(
                acc[:],
                lhsT=codes[:, columns].bitcast(FP8X4),
                lhsT_scale=scales[:, columns],
                rhs=moving.bitcast(FP8X4),
                rhs_scale=moving_scales,
                start=True,
                stop=True,
            )
            return acc

        first_tile, other_tiles = slice(0, 1), slice(1, PACK)

        x_scale_table = load_scales("x_scale_table", x_scales, TOKENS, nc.scalar)
        offs_list = load_list("offs_list", offs)
        k1_list = load_list("k1_list", k1)
        d_scale_table = load_scales("d_scale_table", d_scales, CODEWORDS, nc.sync)
        x_word_table = load_words("x_word_table", x_words, TOKENS)
        k2_list = load_list("k2_list", k2)
        n1_list = load_list("n1_list", n1)
        d_word_table = load_words("d_word_table", d_words, CODEWORDS)
        n2_list = load_list("n2_list", n2)
        n3_list = load_list("n3_list", n3)
        n4_list = load_list("n4_list", n4)
        gains = keep.tile([P, PACK], F32, name="gains")
        nc.gpsimd.dma_start(gains[:], gs.rearrange("(p t) o -> p (t o)", t=PACK))
        placed1 = zeroed_bytes("placed1", 2 * S)
        placed2 = zeroed_bytes("placed2", S)
        warm = keep.tile([P, 2], F32, name="warm")
        nc.vector.memset(warm[:, 0:1], 0.0)
        nc.scalar.activation(warm[:, 1:2], warm[:, 0:1], ACT.Sigmoid)

        picked1 = keep.tile([P, 2 * S], U8, name="picked1", tag="picked1")
        nc.vector.tensor_copy(picked1[:, S:], x_scale_table[:].indirect(offs_list[:]))
        nc.vector.tensor_copy(picked1[:, :S], d_scale_table[:].indirect(k1_list[:]))
        place_scale_rows(placed1, picked1)
        x_codes = keep.tile([P, S], I32, name="x_codes", align_bytes=64)
        gather_words(x_codes, x_word_table, offs_list)
        picked2 = keep.tile([P, S], U8, name="picked2")
        nc.vector.tensor_copy(picked2[:], d_scale_table[:].indirect(k2_list[:]))
        place_scale_rows(placed2, picked2)
        d1_undealt = keep.tile([P, S], I32, name="d1_undealt")
        gather_words(d1_undealt, d_word_table, k1_list)
        d1_scales = keep.tile([P, S], U8, name="d1_scales", align_bytes=64)
        deal_bytes(d1_scales[:], placed1[:, :S], first_tile)
        d1_codes = keep.tile([P, S], I32, name="d1_codes", align_bytes=64)
        deal_words(d1_codes, d1_undealt)
        deal_bytes(d1_scales[:], placed1[:, :S], other_tiles)
        d2_undealt = keep.tile([P, S], I32, name="d2_undealt", tag="picked1")
        gather_words(d2_undealt, d_word_table, k2_list)

        h = {}
        for t in PAIR_ORDER:
            acc = product(t, d1_codes, d1_scales, t, x_codes[:], placed1[:, S:])
            h[t] = keep.tile([P, S], F32, name=f"h{t}", tag=f"h{t}", align_bytes=64)
            nc.scalar.activation(h[t][:], acc[:], ACT.Copy, scale=SIXTEENTH)

        last = PAIR_ORDER[-1]
        h2_windows = {t: keep.tile([P, 2 * S], F32, name=f"h2_window{t}") for t in range(1, PACK)}
        pairs = {t: h2_windows[owner][:, S:] for t, owner in zip(PAIR_ORDER[:-1], range(1, PACK))}
        last_pair = keep.tile([P, S], F32, name="last_pair", tag="last_pair", align_bytes=64)
        pairs[last] = last_pair[:]
        pa = {t: pairs[t][:, halves[0]] for t in PAIR_ORDER}
        pb = {t: pairs[t][:, halves[1]] for t in PAIR_ORDER}
        dt = {}
        z = keep.tile([P, S, PACK], BF16, name="z", align_bytes=64)

        def fetch(dst, t, list_tile):
            nc.vector.tensor_copy(dst[t], h[t][:].indirect(list_tile[:]))

        def put_sum(t):
            dt[t] = keep.tile([P, S], F32, name=f"dt{t}", tag="dt", bufs=DT_BUFFERS)
            nc.vector.tensor_tensor(dt[t][:].indirect(n1_list[:]), pa[t], pb[t], ALU.add)

        def put_product(t):
            nc.vector.tensor_tensor(dt[t][:].indirect(n2_list[:]), pa[t], pb[t], ALU.mult)

        def weigh(t, columns):
            nc.scalar.activation(z[:, columns, t], dt[t][:, columns], ACT.Copy, scale=gains[:, t : t + 1])

        fetch(pa, PAIR_ORDER[0], n1_list)
        fetch(pb, PAIR_ORDER[0], n2_list)
        for t, following in zip(PAIR_ORDER, PAIR_ORDER[1:]):
            fetch(pa, following, n1_list)
            put_sum(t)
            fetch(pb, following, n2_list)
            put_product(t)
            weigh(t, slice(0, S))
        put_sum(last)
        d2_codes = keep.tile([P, S], I32, name="d2_codes", tag=f"h{last}", align_bytes=64)
        deal_words(d2_codes, d2_undealt)
        put_product(last)
        weigh(last, slice(0, Z_SPLIT))
        nc.vector.tensor_scalar(z[:, Z_SPLIT:, last], dt[last][:, Z_SPLIT:], gains[:, last : last + 1], None, ALU.mult)

        d2_scales = keep.tile([P, S], U8, name="d2_scales", tag="last_pair", align_bytes=64)
        deal_bytes(d2_scales[:], placed2[:], first_tile)
        z_codes = keep.tile([P, S], I32, name="z_codes", align_bytes=64)
        z_scales = keep.tile([P, S], U8, name="z_scales", align_bytes=64)
        for half in halves:
            nc.vector.quantize_mx(
                z_codes[:, half].bitcast(FP8X4), z_scales[:, half], z[:, half, :].rearrange("p c t -> p (c t)")
            )
        deal_bytes(d2_scales[:], placed2[:], other_tiles)

        neg_st = [keep.tile([P, S], F32, name=f"neg_st{t}") for t in range(PACK)]

        sigmoid0 = keep.tile([P, S], F32, name="sigmoid0")
        neg_h2_0 = keep.tile([P, S], F32, name="neg_h2_0")
        half_accs = [
            product(PACK + u, d2_codes, d2_scales, 0, z_codes[:, half], z_scales[:, half])
            for u, half in enumerate(halves)
        ]
        for half, acc in zip(halves, half_accs):
            nc.scalar.activation(sigmoid0[:, half], acc[:], ACT.Sigmoid, scale=SIXTEENTH)
            nc.vector.tensor_scalar(neg_h2_0[:, half], acc[:], -SIXTEENTH, None, ALU.mult)
        for u, half in enumerate(halves):
            nc.vector.tensor_tensor(
                neg_st[0][:, half], sigmoid0[:].indirect(half_of(n3_list, u)), neg_h2_0[:, half], ALU.mult
            )

        gate = {t: keep.tile([P, S], F32, name=f"gate{t}", tag=f"gate{t}") for t in range(1, PACK)}

        def leave_bank(t):
            acc = product(t, d2_codes, d2_scales, t, z_codes[:], z_scales[:])
            nc.scalar.activation(h2_windows[t][:, :S], acc[:], ACT.Copy, scale=SIXTEENTH)

        leave_bank(1)
        for t in range(1, PACK):
            if t + 1 < PACK:
                leave_bank(t + 1)
            nc.scalar.activation(gate[t][:], h2_windows[t][:].indirect(n3_list[:]), ACT.Sigmoid)

        twin = {}
        y = [keep.tile([P, PACK, HALF], F32, name=f"y{u}") for u in range(2)]
        y_rounded = [keep.tile([P, HALF, PACK], BF16, name=f"y_rounded{u}", align_bytes=64) for u in range(2)]
        y_codes = keep.tile([P, S], I32, name="y_codes", align_bytes=64)
        y_scales = keep.tile([P, S], U8, name="y_scales", align_bytes=64)
        out_rows = out_0.rearrange("(p t) j -> p t j", t=PACK)
        out_words = out_1[0].rearrange("p n t -> p (n t)").bitcast(I32)

        def apply_gate(t):
            nc.vector.scalar_tensor_tensor(neg_st[t][:], h2_windows[t][:, :S], -1.0, gate[t][:], ALU.mult, ALU.mult)

        def duplicate(t, u, copy, buffer=None):
            twin[t, u] = keep.tile([P, HALF], F32, name=f"twin{t}_{u}", tag=buffer or f"twin{t}_{u}")
            copy(twin[t, u][:], neg_st[t][:, halves[u]])

        def hop(t, u):
            nc.vector.tensor_tensor(y[u][:, t, :], neg_st[t][:].indirect(half_of(n4_list, u)), twin[t, u][:], ALU.subtract)

        def store(u, row_tiles):
            nc.sync.dma_start(out_rows[:, row_tiles, halves[u]], y[u][:, row_tiles, :])

        def round_y(u, columns, copy):
            copy(
                y_rounded[u][:, columns, :].rearrange("p (c i) t -> p c t i", i=LINE),
                y[u][:, :, columns].rearrange("p t (c i) -> p c t i", i=LINE),
            )

        def quantise_y(u):
            half = halves[u]
            nc.vector.quantize_mx(
                y_codes[:, half].bitcast(FP8X4), y_scales[:, half], y_rounded[u][:].rearrange("p c t -> p (c t)")
            )
            nc.sync.dma_start(out_words[:, half], y_codes[:, half])

        low_tiles, high_tiles = slice(0, 2), slice(2, PACK)
        duplicate(0, 0, nc.vector.tensor_copy)
        duplicate(0, 1, nc.vector.tensor_copy)
        hop(0, 0)
        apply_gate(1)
        hop(0, 1)
        duplicate(1, 0, nc.vector.tensor_copy)
        apply_gate(2)
        duplicate(2, 0, nc.scalar.copy)
        duplicate(1, 1, nc.scalar.copy)
        hop(1, 0)
        store(0, low_tiles)
        apply_gate(3)
        duplicate(3, 0, nc.scalar.copy)
        duplicate(2, 1, nc.scalar.copy, buffer="gate3")
        duplicate(3, 1, nc.scalar.copy)
        hop(2, 0)
        hop(1, 1)
        store(1, low_tiles)
        hop(3, 0)
        store(0, high_tiles)
        round_y(0, slice(0, HALF), nc.scalar.copy)
        hop(2, 1)
        hop(3, 1)
        store(1, high_tiles)
        round_y(1, slice(0, Y_SPLIT), nc.scalar.copy)
        round_y(1, slice(Y_SPLIT, HALF), nc.vector.tensor_copy)
        quantise_y(0)
        quantise_y(1)

        for q in range(P // QUADRANT):
            queue = nc.sync if q % 2 else nc.scalar
            queue.dma_start(
                out_2[0][PACK * q : PACK * (q + 1), :].bitcast(I32),
                y_scales[QUADRANT * q : QUADRANT * q + PACK, :].bitcast(I32),
            )
